import numpy as np
import ml_dtypes


def mxq(x, axis, fmt="e4m3"):
    dtype, down = {"e4m3": (ml_dtypes.float8_e4m3fn, 7), "e5m2": (ml_dtypes.float8_e5m2, 14)}[fmt]
    v = np.moveaxis(np.asarray(x, np.float32).astype(ml_dtypes.bfloat16).astype(np.float64), axis, -1)
    blocks = v.reshape(v.shape[:-1] + (-1, 32))
    amax = np.abs(blocks).max(-1, keepdims=True)
    byte = np.maximum(np.where(amax > 0, np.frexp(amax)[1] - 1 + 127, 0) - down, 1)
    scale = np.exp2(byte - 127.0)
    codes = (blocks / scale).astype(np.float32).astype(dtype).astype(np.float64)
    return np.moveaxis((codes * scale).reshape(v.shape), -1, axis)


WIDE = False


def mx_kscale(k):
    if not WIDE:
        return np.ones(k)
    levels = np.array([10, -10, 5, -5, 0])
    if k % 512:
        return np.exp2(np.random.permutation(np.resize(levels, k // 32))).repeat(32)
    a = np.empty((k // 512, 16))
    for p in range(k // 512):
        a[p, :8] = np.random.permutation(np.resize(levels, 8))
        for g in range(8):
            far = levels[np.abs(levels - a[p, g]) >= 10]
            a[p, g + 8] = far[np.random.randint(len(far))]
    return np.exp2(a.ravel()).repeat(32)


def f64(x):
    return np.asarray(x).astype(np.float64)


def striped(idx):
    return np.tile(idx.reshape(-1, 16).T, (8, 1)).astype(np.uint16)


def unstriped(offs):
    return offs[:16].T.reshape(-1).astype(np.int64)


E2M1 = np.array([0.0, 0.5, 1.0, 1.5, 2.0, 3.0, 4.0, 6.0, -0.0, -0.5, -1.0, -1.5, -2.0, -3.0, -4.0, -6.0])


def pack_weight(w, fmt):
    k, n = w.shape
    w = f64(np.asarray(w, np.float32).astype(ml_dtypes.bfloat16)).reshape(k // 32, 32, n)
    amax = np.abs(w).max(1)
    if fmt == "e4m3":
        byte = np.frexp(amax)[1] - 1 + 127 - 7
    else:
        mant, ex = np.frexp(amax / 6.0)
        byte = np.where(mant > 0.5, ex, ex - 1) + 127
    byte = np.clip(np.where(amax > 0, byte, 1), 1, 254)
    scaled = (w * np.exp2(127.0 - byte)[:, None, :]).reshape(k, n).astype(np.float32)
    by_word = np.ascontiguousarray(scaled.reshape(k // 512, 128, 4, n).transpose(0, 1, 3, 2))
    if fmt == "e4m3":
        words = by_word.astype(ml_dtypes.float8_e4m3fn).view(np.uint8)
    else:
        c = by_word.astype(ml_dtypes.float4_e2m1fn).view(np.uint8) & 0xF
        words = (c[..., 0::2] | (c[..., 1::2] << 4)).reshape(k // 512, 128, 2 * n)
    return np.ascontiguousarray(words), np.ascontiguousarray(byte.astype(np.uint8).reshape(k // 512, 16, n))


def unpack_weight(words, scales, fmt):
    g, _, n = scales.shape
    words = np.ascontiguousarray(words).reshape(g, 128, n, -1)
    if fmt == "e4m3":
        vals = words.view(ml_dtypes.float8_e4m3fn).astype(np.float64)
    else:
        nib = np.empty((g, 128, n, 4), np.uint8)
        nib[..., 0::2] = words & 0xF
        nib[..., 1::2] = words >> 4
        vals = E2M1[nib]
    vals = vals * np.repeat(np.exp2(scales.astype(np.float64) - 127.0), 8, axis=1)[..., None]
    return vals.transpose(0, 1, 3, 2).reshape(g * 512, n)


def gelu(v):
    return 0.5 * v * (1.0 + np.tanh(np.sqrt(2.0 / np.pi) * (v + 0.044715 * v**3)))


K, T, E, C, H, TOP, COPIES = 512, 640, 8, 256, 512, 4, 160
PAD = 64


def by_expert(wq, xq):
    return np.concatenate([wq[e].T @ xq[:, e * C:(e + 1) * C] for e in range(E)], axis=1)


def setup_inputs():
    n = np.random.standard_normal
    s = mx_kscale(K)
    u = mx_kscale(H)
    left = TOP * T - E * C - COPIES
    deal = np.repeat(np.arange(E + 2), [C] * E + [COPIES, left]).reshape(TOP, T)[:, np.random.permutation(T)]
    deal = np.take_along_axis(deal, np.argsort(np.random.rand(TOP, T), axis=0), axis=0)
    for _ in range(8):
        s_, t_ = np.random.permutation(T).reshape(2, -1); r = np.random.randint(TOP, size=T // 2); x, y = deal[r, s_].copy(), deal[r, t_].copy()
        ok = ~((deal[:, s_] == y).any(0) | (deal[:, t_] == x).any(0)); deal[r[ok], s_[ok]] = y[ok]; deal[r[ok], t_[ok]] = x[ok]
    order = np.lexsort((np.random.rand(TOP * T), deal.reshape(-1)))[:E * C]
    slot_token = order % T
    pos = np.where(deal == E, E * C + np.arange(T), E * C + T + np.arange(T) % PAD).reshape(-1); pos[order] = np.arange(E * C); pos = pos.reshape(TOP, T)
    g = np.random.uniform(0.5, 1.5, (TOP, T)); g = g / g.sum(0)
    xf = n((K, T))
    x = pack_weight(xf * s[:, None], "e4m3")
    w1 = [pack_weight(m, "e2m1") for m in n((E, K, H)) / np.sqrt(K) / s[None, :, None] * u]
    w2 = [pack_weight(m, "e2m1") for m in n((E, H, K)) / np.sqrt(H) / u[None, :, None]]
    return {
        "x_words": x[0],
        "x_scales": x[1],
        "xr": (xf).astype(np.float32),
        "w1_words": np.stack([m[0] for m in w1]),
        "w1_scales": np.stack([m[1] for m in w1]),
        "w2_words": np.stack([m[0] for m in w2]),
        "w2_scales": np.stack([m[1] for m in w2]),
        "gate": np.stack([np.tile(r, (128, 1)) for r in g]).astype(np.float32),
        "offs": striped(slot_token),
        "pos1": striped(pos[0]),
        "pos2": striped(pos[1]),
        "pos3": striped(pos[2]),
        "pos4": striped(pos[3]),
    }


def reference(x_words, x_scales, xr, w1_words, w1_scales, w2_words, w2_scales, gate, offs, pos1, pos2, pos3, pos4):
    w1 = np.stack([unpack_weight(w1_words[e], w1_scales[e], "e2m1") for e in range(E)])
    w2 = np.stack([unpack_weight(w2_words[e], w2_scales[e], "e2m1") for e in range(E)])
    idx = unstriped(offs)
    xq = unpack_weight(x_words, x_scales, "e4m3")[:, idx]
    h = gelu(by_expert(w1, xq))
    y = by_expert(w2, mxq(h, 0, "e4m3"))
    y = np.concatenate([y, f64(xr), np.zeros((K, PAD))], axis=1)
    out = sum(f64(gate[r, :1]) * y[:, unstriped(p)] for r, p in enumerate((pos1, pos2, pos3, pos4)))
    return out

@@ -1,0 +1,214 @@
+from contextlib import ExitStack
+
+import concourse.mybir as mybir
+from concourse.masks import make_identity
+
+F32 = mybir.dt.float32
+BF16 = mybir.dt.bfloat16
+I32 = mybir.dt.int32
+U32 = mybir.dt.uint32
+U16 = mybir.dt.uint16
+U8 = mybir.dt.uint8
+FP8X4 = mybir.dt.float8_e4m3fn_x4
+FP4X4 = mybir.dt.float4_e2m1fn_x4
+GELU = mybir.ActivationFunctionType.Gelu_apprx_tanh
+MULT = mybir.AluOpType.mult
+ADD = mybir.AluOpType.add
+
+P = 128
+K, T, E, C, H, TOP = 512, 640, 8, 256, 512, 4
+SLOTS = E * C
+ZEROS = 64
+WINDOW = SLOTS + T + ZEROS
+BLOCKS = K // P
+FLOPS = 2 * SLOTS * (K * H + H * K)
+
+VECTOR_H_COPIES = (6, 7,)
+VECTOR_TAIL = 256
+
+
+def load_scale_rows(nc, plane, rows):
+    for q in range(4):
+        nc.sync.dma_start(out=plane[32 * q : 32 * q + 4], in_=rows[4 * q : 4 * q + 4])
+
+
+def tile_moe_cpy_mlp_gelu_kernel(
+    tc, x_words, x_scales, xr, w1_words, w1_scales, w2_words, w2_scales, gate, offs, pos1, pos2, pos3, pos4, out
+):
+    nc = tc.nc
+    with ExitStack() as ctx:
+        keep = ctx.enter_context(tc.tile_pool(name="keep", bufs=1))
+        ring = ctx.enter_context(tc.tile_pool(name="ring", bufs=3))
+        prods = ctx.enter_context(tc.tile_pool(name="prods", bufs=6))
+        acc_banks = ctx.enter_context(tc.psum_pool(name="acc_banks", bufs=4))
+        turn_banks = ctx.enter_context(tc.psum_pool(name="turn_banks", bufs=2))
+        y_banks = ctx.enter_context(tc.psum_pool(name="y_banks", bufs=2))
+
+        slot_list = keep.tile([P, SLOTS // 16], U16, name="slot_list")
+        choice_lists = [keep.tile([P, T // 16], U16, name="choice_list%d" % r) for r in range(TOP)]
+        x_w = keep.tile([P, T], I32, name="x_w", align_bytes=64)
+        x_s = keep.tile([P, T // 4], I32, name="x_s", align_bytes=64)
+        x_s_rows = keep.tile([P, T // 4], I32, name="x_s_rows")
+        w1_w = keep.tile([P, E, 2 * H], U8, name="w1_w", align_bytes=64)
+        w2_w = keep.tile([P, E, 2 * K], U8, name="w2_w", align_bytes=64)
+        w1_s = keep.tile([P, E, H], U8, name="w1_s", align_bytes=64)
+        w2_s = keep.tile([P, E, K], U8, name="w2_s", align_bytes=64)
+        gates = keep.tile([P, TOP, T], F32, name="gates")
+        ys = [keep.tile([P, WINDOW], F32, name="y%d" % b) for b in range(BLOCKS)]
+        ident = keep.tile([P, P], F32, name="ident")
+        zeros = keep.tile([P, ZEROS], F32, name="zeros")
+
+        nc.gpsimd.memset(zeros[:], 0.0)
+        nc.vector.memset(x_s[:], 0)
+        make_identity(nc, ident[:])
+        for b in range(BLOCKS):
+            nc.scalar.activation(ys[b][:, SLOTS + T :], zeros[:], GELU)
+
+        def load_words(tile, words, e0, e1):
+            nc.sync.dma_start(
+                out=tile[:, e0:e1, :].bitcast(I32),
+                in_=words[e0:e1, 0].rearrange("e p b -> p e b").bitcast(I32),
+            )
+
+        load_scale_rows(nc, x_s_rows[:], x_scales[0].bitcast(I32))
+        for q in range(4):
+            nc.vector.tensor_copy(x_s[32 * q : 32 * q + 4], x_s_rows[32 * q : 32 * q + 4])
+        nc.sync.dma_start(slot_list[:], offs)
+        nc.sync.dma_start(out=x_w[:], in_=x_words[0].rearrange("p t d -> p (t d)").bitcast(I32))
+        load_scale_rows(nc, w1_s[:].bitcast(I32), w1_scales[:, 0].rearrange("e r n -> r e n").bitcast(I32))
+        load_words(w1_w, w1_words, 0, 2)
+        load_scale_rows(nc, w2_s[:].bitcast(I32), w2_scales[:, 0].rearrange("e r n -> r e n").bitcast(I32))
+        load_words(w1_w, w1_words, 2, 4)
+        load_words(w2_w, w2_words, 0, 2)
+        load_words(w1_w, w1_words, 4, 8)
+        load_words(w2_w, w2_words, 2, 8)
+        for r, pos in enumerate((pos1, pos2, pos3, pos4)):
+            nc.sync.dma_start(choice_lists[r][:], pos)
+        nc.sync.dma_start(out=ys[0][:, SLOTS : SLOTS + T], in_=xr[0:P, :])
+        nc.sync.dma_start(out=gates[:], in_=gate.rearrange("r p t -> p r t"))
+        for b in range(1, BLOCKS):
+            nc.sync.dma_start(out=ys[b][:, SLOTS : SLOTS + T], in_=xr[b * P : (b + 1) * P, :])
+
+        h_codes = [keep.tile([P, C], U32, name="h_codes%d" % e, align_bytes=64) for e in range(E)]
+        h_scales = [keep.tile([P, C], U8, name="h_scales%d" % e, align_bytes=64) for e in range(E)]
+        slot_w = [keep.tile([P, C], U32, name="slot_w%d" % e, align_bytes=64) for e in range(E)]
+        slot_s = [keep.tile([P, C], U8, name="slot_s%d" % e, align_bytes=64) for e in range(E)]
+
+        def gather_tokens(e):
+            offsets = slot_list[:, e * (C // 16) : (e + 1) * (C // 16)]
+            nc.vector.tensor_copy(slot_w[e][:], x_w[:].bitcast(U32).indirect(offsets))
+            nc.vector.tensor_copy(slot_s[e][:], x_s[:].bitcast(U8).indirect(offsets))
+
+        def second_layer(bank_cols, e, b):
+            nc.tensor.matmul_mx(
+                out=bank_cols,
+                lhsT=w2_w[:, e, 2 * P * b : 2 * P * (b + 1)].bitcast(FP4X4),
+                lhsT_scale=w2_s[:, e, P * b : P * (b + 1)],
+                rhs=h_codes[e][:].bitcast(FP8X4),
+                rhs_scale=h_scales[e][:],
+                start=True,
+                stop=True,
+            )
+
+        def first_layer(e):
+            turned = turn_banks.tile([P, 2, 2, P], F32, name="turned", tag="turn")
+            hidden = []
+            for half in range(2):
+                cols = slice(half * P, (half + 1) * P)
+                acc = acc_banks.tile([P, H], F32, name="acc", tag="acc")
+                nc.tensor.matmul_mx(
+                    out=acc[:],
+                    lhsT=slot_w[e][:, cols].bitcast(FP8X4),
+                    lhsT_scale=slot_s[e][:, cols],
+                    rhs=w1_w[:, e, :].bitcast(FP4X4),
+                    rhs_scale=w1_s[:, e, :],
+                    start=True,
+                    stop=True,
+                )
+                h = ring.tile([P, H], BF16, name="h", tag="h", bufs=4)
+                nc.scalar.activation(
+                    h[:].rearrange("s (u p v) -> s u p v", u=2, v=2),
+                    acc[:].rearrange("s (p u v) -> s u p v", u=2, v=2),
+                    GELU,
+                )
+                hidden.append(h)
+            for half in range(2):
+                pairs = hidden[half][:].bitcast(F32)
+                for u in range(2):
+                    nc.tensor.transpose(turned[:, half, u, :], pairs[:, u * P : (u + 1) * P], ident[:])
+            grouped = ring.tile([P, 4 * C], BF16, name="grouped", tag="grouped", align_bytes=64)
+            dst = grouped[:].bitcast(F32).rearrange("p (a s u) -> p a s u", a=2, u=2)
+            src = turned[:].rearrange("p a u s -> p a s u")
+            if e in VECTOR_H_COPIES:
+                nc.vector.tensor_copy(dst, src)
+            else:
+                nc.scalar.copy(dst, src)
+            return grouped
+
+        def quantize_and_first_block(e, grouped):
+            nc.vector.quantize_mx(out=h_codes[e][:].bitcast(FP8X4), scales=h_scales[e][:], in_=grouped[:])
+            bank = y_banks.tile([P, C], F32, name="y_bank", tag="y")
+            second_layer(bank[:], e, 0)
+            nc.vector.tensor_copy(ys[0][:, e * C : (e + 1) * C], bank[:])
+
+        gather_tokens(0)
+        gather_tokens(1)
+        for e in range(E):
+            grouped = first_layer(e)
+            if e + 2 < E:
+                gather_tokens(e + 2)
+            quantize_and_first_block(e, grouped)
+
+        def fill_block(b):
+            for e in range(0, E, 2):
+                bank = y_banks.tile([P, 2 * C], F32, name="y_bank", tag="y")
+                second_layer(bank[:, :C], e, b)
+                second_layer(bank[:, C:], e + 1, b)
+                nc.scalar.copy(ys[b][:, e * C : (e + 2) * C], bank[:])
+
+        def weighted_choice(b, r, t0, t1):
+            product = prods.tile([P, t1 - t0], F32, name="product", tag="product")
+            offsets = choice_lists[r][:, t0 // 16 : t1 // 16]
+            nc.vector.tensor_tensor(product[:], ys[b][:].indirect(offsets), gates[:, r, t0:t1], MULT)
+            return product
+
+        def combine_on_tensor(b, width):
+            parts = [(t0, min(t0 + 3 * P, width)) for t0 in range(0, width, 3 * P)]
+            sums = [acc_banks.tile([P, t1 - t0], F32, name="sums", tag="acc") for t0, t1 in parts]
+            for r in range(TOP):
+                product = weighted_choice(b, r, 0, width)
+                for (t0, t1), bank in zip(parts, sums):
+                    for t in range(t0, t1, P):
+                        nc.tensor.matmul(
+                            bank[:, t - t0 : t - t0 + P],
+                            lhsT=product[:, t : t + P],
+                            rhs=ident[:],
+                            start=(r == 0 and t == t0),
+                            stop=(r == TOP - 1 and t + P == t1),
+                            is_transpose=True,
+                        )
+            result = ring.tile([P, width], F32, name="result", tag="result")
+            for (t0, t1), bank in zip(parts, sums):
+                by_token = ring.tile([P, t1 - t0], F32, name="by_token", tag="by_token")
+                nc.scalar.copy(by_token[:], bank[:])
+                back = turn_banks.tile([P, t1 - t0], F32, name="back", tag="turn")
+                for t in range(0, t1 - t0, P):
+                    nc.tensor.transpose(back[:, t : t + P], by_token[:, t : t + P], ident[:])
+                nc.scalar.copy(result[:, t0:t1], back[:])
+            nc.sync.dma_start(out=out[b * P : (b + 1) * P, :width], in_=result[:])
+
+        def combine_on_vector(b, t0):
+            p1 = weighted_choice(b, 0, t0, T)
+            p2 = weighted_choice(b, 1, t0, T)
+            p3 = weighted_choice(b, 2, t0, T)
+            nc.vector.tensor_tensor(p1[:], p1[:], p2[:], ADD)
+            p4 = weighted_choice(b, 3, t0, T)
+            nc.vector.tensor_tensor(p1[:], p1[:], p3[:], ADD)
+            nc.vector.tensor_tensor(p1[:], p1[:], p4[:], ADD)
+            nc.sync.dma_start(out=out[b * P : (b + 1) * P, t0:], in_=p1[:])
+
+        for b in range(BLOCKS - 1):
+            fill_block(b + 1)
+            combine_on_tensor(b, T)
+        combine_on_tensor(BLOCKS - 1, T - VECTOR_TAIL)
+        combine_on_vector(BLOCKS - 1, T - VECTOR_TAIL)

@@ -23,13 +23,13 @@ WINDOW = SLOTS + T + ZEROS
 BLOCKS = K // P
 FLOPS = 2 * SLOTS * (K * H + H * K)
 
-VECTOR_H_COPIES = (6, 7,)
+VECTOR_H_COPIES = (4, 5, 6,)
 VECTOR_TAIL = 256
 
 
-def load_scale_rows(nc, plane, rows):
-    for q in range(4):
-        nc.sync.dma_start(out=plane[32 * q : 32 * q + 4], in_=rows[4 * q : 4 * q + 4])
+def load_scale_rows(queues, plane, rows):
+    for q, queue in enumerate(queues):
+        queue.dma_start(out=plane[32 * q : 32 * q + 4], in_=rows[4 * q : 4 * q + 4])
 
 
 def tile_moe_cpy_mlp_gelu_kernel(
@@ -40,17 +40,16 @@ def tile_moe_cpy_mlp_gelu_kernel(
         keep = ctx.enter_context(tc.tile_pool(name="keep", bufs=1))
         ring = ctx.enter_context(tc.tile_pool(name="ring", bufs=3))
         prods = ctx.enter_context(tc.tile_pool(name="prods", bufs=6))
-        acc_banks = ctx.enter_context(tc.psum_pool(name="acc_banks", bufs=4))
         turn_banks = ctx.enter_context(tc.psum_pool(name="turn_banks", bufs=2))
-        y_banks = ctx.enter_context(tc.psum_pool(name="y_banks", bufs=2))
+        sum_banks_even = ctx.enter_context(tc.psum_pool(name="sum_banks_even", bufs=2))
 
         slot_list = keep.tile([P, SLOTS // 16], U16, name="slot_list")
         choice_lists = [keep.tile([P, T // 16], U16, name="choice_list%d" % r) for r in range(TOP)]
         x_w = keep.tile([P, T], I32, name="x_w", align_bytes=64)
         x_s = keep.tile([P, T // 4], I32, name="x_s", align_bytes=64)
         x_s_rows = keep.tile([P, T // 4], I32, name="x_s_rows")
-        w1_w = keep.tile([P, E, 2 * H], U8, name="w1_w", align_bytes=64)
-        w2_w = keep.tile([P, E, 2 * K], U8, name="w2_w", align_bytes=64)
+        w1_w = [keep.tile([P, 2, 2 * H], U8, name="w1_w%d" % i, align_bytes=64) for i in range(E // 2)]
+        w2_w = [keep.tile([P, 2, 2 * K], U8, name="w2_w%d" % i, align_bytes=64) for i in range(E // 2)]
         w1_s = keep.tile([P, E, H], U8, name="w1_s", align_bytes=64)
         w2_s = keep.tile([P, E, K], U8, name="w2_s", align_bytes=64)
         gates = keep.tile([P, TOP, T], F32, name="gates")
@@ -58,30 +57,32 @@ def tile_moe_cpy_mlp_gelu_kernel(
         ident = keep.tile([P, P], F32, name="ident")
         zeros = keep.tile([P, ZEROS], F32, name="zeros")
 
-        nc.gpsimd.memset(zeros[:], 0.0)
         nc.vector.memset(x_s[:], 0)
+        nc.gpsimd.memset(zeros[:], 0.0)
+
+        def load_words(queue, tiles, words, pair):
+            queue.dma_start(
+                out=tiles[pair][:].bitcast(I32),
+                in_=words[2 * pair : 2 * pair + 2, 0].rearrange("e p b -> p e b").bitcast(I32),
+            )
+
+        load_scale_rows((nc.sync, nc.scalar, nc.sync, nc.sync), x_s_rows[:], x_scales[0].bitcast(I32))
+        for q in range(4):
+            nc.vector.tensor_copy(x_s[32 * q : 32 * q + 4], x_s_rows[32 * q : 32 * q + 4])
+        nc.sync.dma_start(out=x_w[:], in_=x_words[0].rearrange("p t d -> p (t d)").bitcast(I32))
+        nc.sync.dma_start(slot_list[:], offs)
+        load_scale_rows((nc.scalar,) * 4, w1_s[:].bitcast(I32), w1_scales[:, 0].rearrange("e r n -> r e n").bitcast(I32))
+        load_words(nc.gpsimd, w1_w, w1_words, 0)
         make_identity(nc, ident[:])
         for b in range(BLOCKS):
             nc.scalar.activation(ys[b][:, SLOTS + T :], zeros[:], GELU)
-
-        def load_words(tile, words, e0, e1):
-            nc.sync.dma_start(
-                out=tile[:, e0:e1, :].bitcast(I32),
-                in_=words[e0:e1, 0].rearrange("e p b -> p e b").bitcast(I32),
-            )
-
-        load_scale_rows(nc, x_s_rows[:], x_scales[0].bitcast(I32))
-        for q in range(4):
-            nc.vector.tensor_copy(x_s[32 * q : 32 * q + 4], x_s_rows[32 * q : 32 * q + 4])
-        nc.sync.dma_start(slot_list[:], offs)
-        nc.sync.dma_start(out=x_w[:], in_=x_words[0].rearrange("p t d -> p (t d)").bitcast(I32))
-        load_scale_rows(nc, w1_s[:].bitcast(I32), w1_scales[:, 0].rearrange("e r n -> r e n").bitcast(I32))
-        load_words(w1_w, w1_words, 0, 2)
-        load_scale_rows(nc, w2_s[:].bitcast(I32), w2_scales[:, 0].rearrange("e r n -> r e n").bitcast(I32))
-        load_words(w1_w, w1_words, 2, 4)
-        load_words(w2_w, w2_words, 0, 2)
-        load_words(w1_w, w1_words, 4, 8)
-        load_words(w2_w, w2_words, 2, 8)
+        load_words(nc.sync, w1_w, w1_words, 1)
+        load_scale_rows((nc.sync,) * 4, w2_s[:].bitcast(I32), w2_scales[:, 0].rearrange("e r n -> r e n").bitcast(I32))
+        load_words(nc.sync, w2_w, w2_words, 0)
+        load_words(nc.sync, w1_w, w1_words, 2)
+        load_words(nc.sync, w1_w, w1_words, 3)
+        for pair in range(1, E // 2):
+            load_words(nc.sync, w2_w, w2_words, pair)
         for r, pos in enumerate((pos1, pos2, pos3, pos4)):
             nc.sync.dma_start(choice_lists[r][:], pos)
         nc.sync.dma_start(out=ys[0][:, SLOTS : SLOTS + T], in_=xr[0:P, :])
@@ -102,7 +103,7 @@ def tile_moe_cpy_mlp_gelu_kernel(
         def second_layer(bank_cols, e, b):
             nc.tensor.matmul_mx(
                 out=bank_cols,
-                lhsT=w2_w[:, e, 2 * P * b : 2 * P * (b + 1)].bitcast(FP4X4),
+                lhsT=w2_w[e // 2][:, e % 2, 2 * P * b : 2 * P * (b + 1)].bitcast(FP4X4),
                 lhsT_scale=w2_s[:, e, P * b : P * (b + 1)],
                 rhs=h_codes[e][:].bitcast(FP8X4),
                 rhs_scale=h_scales[e][:],
@@ -110,7 +111,7 @@ def tile_moe_cpy_mlp_gelu_kernel(
                 stop=True,
             )
 
-        def first_layer(e):
+        def first_layer(e, acc_banks):
             turned = turn_banks.tile([P, 2, 2, P], F32, name="turned", tag="turn")
             hidden = []
             for half in range(2):
@@ -120,12 +121,12 @@ def tile_moe_cpy_mlp_gelu_kernel(
                     out=acc[:],
                     lhsT=slot_w[e][:, cols].bitcast(FP8X4),
                     lhsT_scale=slot_s[e][:, cols],
-                    rhs=w1_w[:, e, :].bitcast(FP4X4),
+                    rhs=w1_w[e // 2][:, e % 2, :].bitcast(FP4X4),
                     rhs_scale=w1_s[:, e, :],
                     start=True,
                     stop=True,
                 )
-                h = ring.tile([P, H], BF16, name="h", tag="h", bufs=4)
+                h = ring.tile([P, H], BF16, name="h", tag="h", bufs=8)
                 nc.scalar.activation(
                     h[:].rearrange("s (u p v) -> s u p v", u=2, v=2),
                     acc[:].rearrange("s (p u v) -> s u p v", u=2, v=2),
@@ -136,7 +137,7 @@ def tile_moe_cpy_mlp_gelu_kernel(
                 pairs = hidden[half][:].bitcast(F32)
                 for u in range(2):
                     nc.tensor.transpose(turned[:, half, u, :], pairs[:, u * P : (u + 1) * P], ident[:])
-            grouped = ring.tile([P, 4 * C], BF16, name="grouped", tag="grouped", align_bytes=64)
+            grouped = ring.tile([P, 4 * C], BF16, name="grouped", tag="grouped", bufs=E, align_bytes=64)
             dst = grouped[:].bitcast(F32).rearrange("p (a s u) -> p a s u", a=2, u=2)
             src = turned[:].rearrange("p a u s -> p a s u")
             if e in VECTOR_H_COPIES:
@@ -145,26 +146,31 @@ def tile_moe_cpy_mlp_gelu_kernel(
                 nc.scalar.copy(dst, src)
             return grouped
 
-        def quantize_and_first_block(e, grouped):
-            nc.vector.quantize_mx(out=h_codes[e][:].bitcast(FP8X4), scales=h_scales[e][:], in_=grouped[:])
-            bank = y_banks.tile([P, C], F32, name="y_bank", tag="y")
-            second_layer(bank[:], e, 0)
-            nc.vector.tensor_copy(ys[0][:, e * C : (e + 1) * C], bank[:])
-
-        gather_tokens(0)
-        gather_tokens(1)
         for e in range(E):
-            grouped = first_layer(e)
-            if e + 2 < E:
-                gather_tokens(e + 2)
-            quantize_and_first_block(e, grouped)
+            gather_tokens(e)
+        with tc.psum_pool(name="acc_banks", bufs=4) as acc_banks:
+            for e in range(E):
+                grouped = first_layer(e, acc_banks)
+                nc.vector.quantize_mx(out=h_codes[e][:].bitcast(FP8X4), scales=h_scales[e][:], in_=grouped[:])
+
+        y_banks = ctx.enter_context(tc.psum_pool(name="y_banks", bufs=2))
+        sum_banks_odd = ctx.enter_context(tc.psum_pool(name="sum_banks_odd", bufs=2))
+
+        def fill(b, e0, e1, copy):
+            bank = y_banks.tile([P, (e1 - e0) * C], F32, name="y_bank", tag="y")
+            for e in range(e0, e1):
+                second_layer(bank[:, (e - e0) * C : (e - e0 + 1) * C], e, b)
+            copy(ys[b][:, e0 * C : e1 * C], bank[:])
 
         def fill_block(b):
             for e in range(0, E, 2):
-                bank = y_banks.tile([P, 2 * C], F32, name="y_bank", tag="y")
-                second_layer(bank[:, :C], e, b)
-                second_layer(bank[:, C:], e + 1, b)
-                nc.scalar.copy(ys[b][:, e * C : (e + 2) * C], bank[:])
+                fill(b, e, e + 2, nc.scalar.copy)
+
+        fill(0, 0, 2, nc.scalar.copy)
+        fill(0, 2, 4, nc.vector.tensor_copy)
+        fill(0, 4, 6, nc.scalar.copy)
+        fill(0, 6, 7, nc.scalar.copy)
+        fill(0, 7, 8, nc.vector.tensor_copy)
 
         def weighted_choice(b, r, t0, t1):
             product = prods.tile([P, t1 - t0], F32, name="product", tag="product")
@@ -174,7 +180,8 @@ def tile_moe_cpy_mlp_gelu_kernel(
 
         def combine_on_tensor(b, width):
             parts = [(t0, min(t0 + 3 * P, width)) for t0 in range(0, width, 3 * P)]
-            sums = [acc_banks.tile([P, t1 - t0], F32, name="sums", tag="acc") for t0, t1 in parts]
+            sum_banks = sum_banks_odd if b % 2 else sum_banks_even
+            sums = [sum_banks.tile([P, t1 - t0], F32, name="sums", tag="acc") for t0, t1 in parts]
             for r in range(TOP):
                 product = weighted_choice(b, r, 0, width)
                 for (t0, t1), bank in zip(parts, sums):

@@ -24,6 +24,7 @@ BLOCKS = K // P
 FLOPS = 2 * SLOTS * (K * H + H * K)
 
 VECTOR_H_COPIES = (4, 5, 6,)
+GATHER_GROUPS = (1, 1, 2, 3, 3, 3, 3)
 VECTOR_TAIL = 256
 
 
@@ -41,7 +42,6 @@ def tile_moe_cpy_mlp_gelu_kernel(
         ring = ctx.enter_context(tc.tile_pool(name="ring", bufs=3))
         prods = ctx.enter_context(tc.tile_pool(name="prods", bufs=6))
         turn_banks = ctx.enter_context(tc.psum_pool(name="turn_banks", bufs=2))
-        sum_banks_even = ctx.enter_context(tc.psum_pool(name="sum_banks_even", bufs=2))
 
         slot_list = keep.tile([P, SLOTS // 16], U16, name="slot_list")
         choice_lists = [keep.tile([P, T // 16], U16, name="choice_list%d" % r) for r in range(TOP)]
@@ -71,7 +71,7 @@ def tile_moe_cpy_mlp_gelu_kernel(
             nc.vector.tensor_copy(x_s[32 * q : 32 * q + 4], x_s_rows[32 * q : 32 * q + 4])
         nc.sync.dma_start(out=x_w[:], in_=x_words[0].rearrange("p t d -> p (t d)").bitcast(I32))
         nc.sync.dma_start(slot_list[:], offs)
-        load_scale_rows((nc.scalar,) * 4, w1_s[:].bitcast(I32), w1_scales[:, 0].rearrange("e r n -> r e n").bitcast(I32))
+        load_scale_rows((nc.scalar, nc.scalar, nc.sync, nc.sync), w1_s[:].bitcast(I32), w1_scales[:, 0].rearrange("e r n -> r e n").bitcast(I32))
         load_words(nc.gpsimd, w1_w, w1_words, 0)
         make_identity(nc, ident[:])
         for b in range(BLOCKS):
@@ -92,13 +92,16 @@ def tile_moe_cpy_mlp_gelu_kernel(
 
         h_codes = [keep.tile([P, C], U32, name="h_codes%d" % e, align_bytes=64) for e in range(E)]
         h_scales = [keep.tile([P, C], U8, name="h_scales%d" % e, align_bytes=64) for e in range(E)]
-        slot_w = [keep.tile([P, C], U32, name="slot_w%d" % e, align_bytes=64) for e in range(E)]
-        slot_s = [keep.tile([P, C], U8, name="slot_s%d" % e, align_bytes=64) for e in range(E)]
+        slot_groups = []
 
-        def gather_tokens(e):
-            offsets = slot_list[:, e * (C // 16) : (e + 1) * (C // 16)]
-            nc.vector.tensor_copy(slot_w[e][:], x_w[:].bitcast(U32).indirect(offsets))
-            nc.vector.tensor_copy(slot_s[e][:], x_s[:].bitcast(U8).indirect(offsets))
+        def gather_tokens(first, count):
+            words = keep.tile([P, count * P], U32, name="slot_w%d" % first, align_bytes=64)
+            scales = keep.tile([P, count * P], U8, name="slot_s%d" % first, align_bytes=64)
+            offsets = slot_list[:, first * P // 16 : (first + count) * P // 16]
+            nc.vector.tensor_copy(words[:], x_w[:].bitcast(U32).indirect(offsets))
+            nc.vector.tensor_copy(scales[:], x_s[:].bitcast(U8).indirect(offsets))
+            for g in range(count):
+                slot_groups.append((words[:, g * P : (g + 1) * P], scales[:, g * P : (g + 1) * P]))
 
         def second_layer(bank_cols, e, b):
             nc.tensor.matmul_mx(
@@ -115,12 +118,12 @@ def tile_moe_cpy_mlp_gelu_kernel(
             turned = turn_banks.tile([P, 2, 2, P], F32, name="turned", tag="turn")
             hidden = []
             for half in range(2):
-                cols = slice(half * P, (half + 1) * P)
+                words, scales = slot_groups[2 * e + half]
                 acc = acc_banks.tile([P, H], F32, name="acc", tag="acc")
                 nc.tensor.matmul_mx(
                     out=acc[:],
-                    lhsT=slot_w[e][:, cols].bitcast(FP8X4),
-                    lhsT_scale=slot_s[e][:, cols],
+                    lhsT=words.bitcast(FP8X4),
+                    lhsT_scale=scales,
                     rhs=w1_w[e // 2][:, e % 2, :].bitcast(FP4X4),
                     rhs_scale=w1_s[:, e, :],
                     start=True,
@@ -146,31 +149,38 @@ def tile_moe_cpy_mlp_gelu_kernel(
                 nc.scalar.copy(dst, src)
             return grouped
 
-        for e in range(E):
-            gather_tokens(e)
-        with tc.psum_pool(name="acc_banks", bufs=4) as acc_banks:
-            for e in range(E):
-                grouped = first_layer(e, acc_banks)
-                nc.vector.quantize_mx(out=h_codes[e][:].bitcast(FP8X4), scales=h_scales[e][:], in_=grouped[:])
+        for count in GATHER_GROUPS:
+            gather_tokens(len(slot_groups), count)
 
-        y_banks = ctx.enter_context(tc.psum_pool(name="y_banks", bufs=2))
-        sum_banks_odd = ctx.enter_context(tc.psum_pool(name="sum_banks_odd", bufs=2))
-
-        def fill(b, e0, e1, copy):
-            bank = y_banks.tile([P, (e1 - e0) * C], F32, name="y_bank", tag="y")
+        def fill(banks, b, e0, e1, copy):
+            bank = banks.tile([P, (e1 - e0) * C], F32, name="y_bank", tag="y")
             for e in range(e0, e1):
                 second_layer(bank[:, (e - e0) * C : (e - e0 + 1) * C], e, b)
             copy(ys[b][:, e0 * C : e1 * C], bank[:])
 
         def fill_block(b):
             for e in range(0, E, 2):
-                fill(b, e, e + 2, nc.scalar.copy)
+                fill(y_banks, b, e, e + 2, nc.scalar.copy)
 
-        fill(0, 0, 2, nc.scalar.copy)
-        fill(0, 2, 4, nc.vector.tensor_copy)
-        fill(0, 4, 6, nc.scalar.copy)
-        fill(0, 6, 7, nc.scalar.copy)
-        fill(0, 7, 8, nc.vector.tensor_copy)
+        def hidden_codes(e, acc_banks):
+            grouped = first_layer(e, acc_banks)
+            nc.vector.quantize_mx(out=h_codes[e][:].bitcast(FP8X4), scales=h_scales[e][:], in_=grouped[:])
+
+        with tc.psum_pool(name="acc_banks", bufs=4) as acc_banks:
+            with tc.psum_pool(name="acc_banks_early", bufs=2) as acc_banks_early:
+                for e in range(E - 1):
+                    hidden_codes(e, acc_banks if e % 3 else acc_banks_early)
+            with tc.psum_pool(name="first_banks", bufs=2) as first_banks:
+                hidden_codes(E - 1, acc_banks)
+                fill(first_banks, 0, 0, 2, nc.scalar.copy)
+                fill(first_banks, 0, 2, 4, nc.vector.tensor_copy)
+                fill(first_banks, 0, 4, 6, nc.scalar.copy)
+                fill(first_banks, 0, 6, 7, nc.scalar.copy)
+                fill(first_banks, 0, 7, 8, nc.vector.tensor_copy)
+
+        sum_banks_odd = ctx.enter_context(tc.psum_pool(name="sum_banks_odd", bufs=2))
+        sum_banks_even = ctx.enter_context(tc.psum_pool(name="sum_banks_even", bufs=2))
+        y_banks = ctx.enter_context(tc.psum_pool(name="y_banks", bufs=2))
 
         def weighted_choice(b, r, t0, t1):
             product = prods.tile([P, t1 - t0], F32, name="product", tag="product")

from contextlib import ExitStack

import concourse.mybir as mybir
from concourse.masks import make_identity

F32 = mybir.dt.float32
BF16 = mybir.dt.bfloat16
I32 = mybir.dt.int32
U32 = mybir.dt.uint32
U16 = mybir.dt.uint16
U8 = mybir.dt.uint8
FP8X4 = mybir.dt.float8_e4m3fn_x4
FP4X4 = mybir.dt.float4_e2m1fn_x4
GELU = mybir.ActivationFunctionType.Gelu_apprx_tanh
MULT = mybir.AluOpType.mult
ADD = mybir.AluOpType.add

P = 128
K, T, E, C, H, TOP = 512, 640, 8, 256, 512, 4
SLOTS = E * C
ZEROS = 64
WINDOW = SLOTS + T + ZEROS
BLOCKS = K // P
FLOPS = 2 * SLOTS * (K * H + H * K)

VECTOR_H_COPIES = (4, 5, 6,)
GATHER_GROUPS = (1, 1, 2, 3, 3, 3, 3)
VECTOR_TAIL = 256


def load_scale_rows(queues, plane, rows):
    for q, queue in enumerate(queues):
        queue.dma_start(out=plane[32 * q : 32 * q + 4], in_=rows[4 * q : 4 * q + 4])


def tile_moe_cpy_mlp_gelu_kernel(
    tc, x_words, x_scales, xr, w1_words, w1_scales, w2_words, w2_scales, gate, offs, pos1, pos2, pos3, pos4, out
):
    nc = tc.nc
    with ExitStack() as ctx:
        keep = ctx.enter_context(tc.tile_pool(name="keep", bufs=1))
        ring = ctx.enter_context(tc.tile_pool(name="ring", bufs=3))
        prods = ctx.enter_context(tc.tile_pool(name="prods", bufs=6))
        turn_banks = ctx.enter_context(tc.psum_pool(name="turn_banks", bufs=2))

        slot_list = keep.tile([P, SLOTS // 16], U16, name="slot_list")
        choice_lists = [keep.tile([P, T // 16], U16, name="choice_list%d" % r) for r in range(TOP)]
        x_w = keep.tile([P, T], I32, name="x_w", align_bytes=64)
        x_s = keep.tile([P, T // 4], I32, name="x_s", align_bytes=64)
        x_s_rows = keep.tile([P, T // 4], I32, name="x_s_rows")
        w1_w = [keep.tile([P, 2, 2 * H], U8, name="w1_w%d" % i, align_bytes=64) for i in range(E // 2)]
        w2_w = [keep.tile([P, 2, 2 * K], U8, name="w2_w%d" % i, align_bytes=64) for i in range(E // 2)]
        w1_s = keep.tile([P, E, H], U8, name="w1_s", align_bytes=64)
        w2_s = keep.tile([P, E, K], U8, name="w2_s", align_bytes=64)
        gates = keep.tile([P, TOP, T], F32, name="gates")
        ys = [keep.tile([P, WINDOW], F32, name="y%d" % b) for b in range(BLOCKS)]
        ident = keep.tile([P, P], F32, name="ident")
        zeros = keep.tile([P, ZEROS], F32, name="zeros")

        nc.vector.memset(x_s[:], 0)
        nc.gpsimd.memset(zeros[:], 0.0)

        def load_words(queue, tiles, words, pair):
            queue.dma_start(
                out=tiles[pair][:].bitcast(I32),
                in_=words[2 * pair : 2 * pair + 2, 0].rearrange("e p b -> p e b").bitcast(I32),
            )

        load_scale_rows((nc.sync, nc.scalar, nc.sync, nc.sync), x_s_rows[:], x_scales[0].bitcast(I32))
        for q in range(4):
            nc.vector.tensor_copy(x_s[32 * q : 32 * q + 4], x_s_rows[32 * q : 32 * q + 4])
        nc.sync.dma_start(out=x_w[:], in_=x_words[0].rearrange("p t d -> p (t d)").bitcast(I32))
        nc.sync.dma_start(slot_list[:], offs)
        load_scale_rows((nc.scalar, nc.scalar, nc.sync, nc.sync), w1_s[:].bitcast(I32), w1_scales[:, 0].rearrange("e r n -> r e n").bitcast(I32))
        load_words(nc.gpsimd, w1_w, w1_words, 0)
        make_identity(nc, ident[:])
        for b in range(BLOCKS):
            nc.scalar.activation(ys[b][:, SLOTS + T :], zeros[:], GELU)
        load_words(nc.sync, w1_w, w1_words, 1)
        load_scale_rows((nc.sync,) * 4, w2_s[:].bitcast(I32), w2_scales[:, 0].rearrange("e r n -> r e n").bitcast(I32))
        load_words(nc.sync, w2_w, w2_words, 0)
        load_words(nc.sync, w1_w, w1_words, 2)
        load_words(nc.sync, w1_w, w1_words, 3)
        for pair in range(1, E // 2):
            load_words(nc.sync, w2_w, w2_words, pair)
        for r, pos in enumerate((pos1, pos2, pos3, pos4)):
            nc.sync.dma_start(choice_lists[r][:], pos)
        nc.sync.dma_start(out=ys[0][:, SLOTS : SLOTS + T], in_=xr[0:P, :])
        nc.sync.dma_start(out=gates[:], in_=gate.rearrange("r p t -> p r t"))
        for b in range(1, BLOCKS):
            nc.sync.dma_start(out=ys[b][:, SLOTS : SLOTS + T], in_=xr[b * P : (b + 1) * P, :])

        h_codes = [keep.tile([P, C], U32, name="h_codes%d" % e, align_bytes=64) for e in range(E)]
        h_scales = [keep.tile([P, C], U8, name="h_scales%d" % e, align_bytes=64) for e in range(E)]
        slot_groups = []

        def gather_tokens(first, count):
            words = keep.tile([P, count * P], U32, name="slot_w%d" % first, align_bytes=64)
            scales = keep.tile([P, count * P], U8, name="slot_s%d" % first, align_bytes=64)
            offsets = slot_list[:, first * P // 16 : (first + count) * P // 16]
            nc.vector.tensor_copy(words[:], x_w[:].bitcast(U32).indirect(offsets))
            nc.vector.tensor_copy(scales[:], x_s[:].bitcast(U8).indirect(offsets))
            for g in range(count):
                slot_groups.append((words[:, g * P : (g + 1) * P], scales[:, g * P : (g + 1) * P]))

        def second_layer(bank_cols, e, b):
            nc.tensor.matmul_mx(
                out=bank_cols,
                lhsT=w2_w[e // 2][:, e % 2, 2 * P * b : 2 * P * (b + 1)].bitcast(FP4X4),
                lhsT_scale=w2_s[:, e, P * b : P * (b + 1)],
                rhs=h_codes[e][:].bitcast(FP8X4),
                rhs_scale=h_scales[e][:],
                start=True,
                stop=True,
            )

        def first_layer(e, acc_banks):
            turned = turn_banks.tile([P, 2, 2, P], F32, name="turned", tag="turn")
            hidden = []
            for half in range(2):
                words, scales = slot_groups[2 * e + half]
                acc = acc_banks.tile([P, H], F32, name="acc", tag="acc")
                nc.tensor.matmul_mx(
                    out=acc[:],
                    lhsT=words.bitcast(FP8X4),
                    lhsT_scale=scales,
                    rhs=w1_w[e // 2][:, e % 2, :].bitcast(FP4X4),
                    rhs_scale=w1_s[:, e, :],
                    start=True,
                    stop=True,
                )
                h = ring.tile([P, H], BF16, name="h", tag="h", bufs=8)
                nc.scalar.activation(
                    h[:].rearrange("s (u p v) -> s u p v", u=2, v=2),
                    acc[:].rearrange("s (p u v) -> s u p v", u=2, v=2),
                    GELU,
                )
                hidden.append(h)
            for half in range(2):
                pairs = hidden[half][:].bitcast(F32)
                for u in range(2):
                    nc.tensor.transpose(turned[:, half, u, :], pairs[:, u * P : (u + 1) * P], ident[:])
            grouped = ring.tile([P, 4 * C], BF16, name="grouped", tag="grouped", bufs=E, align_bytes=64)
            dst = grouped[:].bitcast(F32).rearrange("p (a s u) -> p a s u", a=2, u=2)
            src = turned[:].rearrange("p a u s -> p a s u")
            if e in VECTOR_H_COPIES:
                nc.vector.tensor_copy(dst, src)
            else:
                nc.scalar.copy(dst, src)
            return grouped

        for count in GATHER_GROUPS:
            gather_tokens(len(slot_groups), count)

        def fill(banks, b, e0, e1, copy):
            bank = banks.tile([P, (e1 - e0) * C], F32, name="y_bank", tag="y")
            for e in range(e0, e1):
                second_layer(bank[:, (e - e0) * C : (e - e0 + 1) * C], e, b)
            copy(ys[b][:, e0 * C : e1 * C], bank[:])

        def fill_block(b):
            for e in range(0, E, 2):
                fill(y_banks, b, e, e + 2, nc.scalar.copy)

        def hidden_codes(e, acc_banks):
            grouped = first_layer(e, acc_banks)
            nc.vector.quantize_mx(out=h_codes[e][:].bitcast(FP8X4), scales=h_scales[e][:], in_=grouped[:])

        with tc.psum_pool(name="acc_banks", bufs=4) as acc_banks:
            with tc.psum_pool(name="acc_banks_early", bufs=2) as acc_banks_early:
                for e in range(E - 1):
                    hidden_codes(e, acc_banks if e % 3 else acc_banks_early)
            with tc.psum_pool(name="first_banks", bufs=2) as first_banks:
                hidden_codes(E - 1, acc_banks)
                fill(first_banks, 0, 0, 2, nc.scalar.copy)
                fill(first_banks, 0, 2, 4, nc.vector.tensor_copy)
                fill(first_banks, 0, 4, 6, nc.scalar.copy)
                fill(first_banks, 0, 6, 7, nc.scalar.copy)
                fill(first_banks, 0, 7, 8, nc.vector.tensor_copy)

        sum_banks_odd = ctx.enter_context(tc.psum_pool(name="sum_banks_odd", bufs=2))
        sum_banks_even = ctx.enter_context(tc.psum_pool(name="sum_banks_even", bufs=2))
        y_banks = ctx.enter_context(tc.psum_pool(name="y_banks", bufs=2))

        def weighted_choice(b, r, t0, t1):
            product = prods.tile([P, t1 - t0], F32, name="product", tag="product")
            offsets = choice_lists[r][:, t0 // 16 : t1 // 16]
            nc.vector.tensor_tensor(product[:], ys[b][:].indirect(offsets), gates[:, r, t0:t1], MULT)
            return product

        def combine_on_tensor(b, width):
            parts = [(t0, min(t0 + 3 * P, width)) for t0 in range(0, width, 3 * P)]
            sum_banks = sum_banks_odd if b % 2 else sum_banks_even
            sums = [sum_banks.tile([P, t1 - t0], F32, name="sums", tag="acc") for t0, t1 in parts]
            for r in range(TOP):
                product = weighted_choice(b, r, 0, width)
                for (t0, t1), bank in zip(parts, sums):
                    for t in range(t0, t1, P):
                        nc.tensor.matmul(
                            bank[:, t - t0 : t - t0 + P],
                            lhsT=product[:, t : t + P],
                            rhs=ident[:],
                            start=(r == 0 and t == t0),
                            stop=(r == TOP - 1 and t + P == t1),
                            is_transpose=True,
                        )
            result = ring.tile([P, width], F32, name="result", tag="result")
            for (t0, t1), bank in zip(parts, sums):
                by_token = ring.tile([P, t1 - t0], F32, name="by_token", tag="by_token")
                nc.scalar.copy(by_token[:], bank[:])
                back = turn_banks.tile([P, t1 - t0], F32, name="back", tag="turn")
                for t in range(0, t1 - t0, P):
                    nc.tensor.transpose(back[:, t : t + P], by_token[:, t : t + P], ident[:])
                nc.scalar.copy(result[:, t0:t1], back[:])
            nc.sync.dma_start(out=out[b * P : (b + 1) * P, :width], in_=result[:])

        def combine_on_vector(b, t0):
            p1 = weighted_choice(b, 0, t0, T)
            p2 = weighted_choice(b, 1, t0, T)
            p3 = weighted_choice(b, 2, t0, T)
            nc.vector.tensor_tensor(p1[:], p1[:], p2[:], ADD)
            p4 = weighted_choice(b, 3, t0, T)
            nc.vector.tensor_tensor(p1[:], p1[:], p3[:], ADD)
            nc.vector.tensor_tensor(p1[:], p1[:], p4[:], ADD)
            nc.sync.dma_start(out=out[b * P : (b + 1) * P, t0:], in_=p1[:])

        for b in range(BLOCKS - 1):
            fill_block(b + 1)
            combine_on_tensor(b, T)
        combine_on_tensor(BLOCKS - 1, T - VECTOR_TAIL)
        combine_on_vector(BLOCKS - 1, T - VECTOR_TAIL)
